import numpy as np
import ml_dtypes


def mxq(x, axis, fmt="e4m3"):
    dtype, down = {"e4m3": (ml_dtypes.float8_e4m3fn, 7), "e5m2": (ml_dtypes.float8_e5m2, 14)}[fmt]
    v = np.moveaxis(np.asarray(x, np.float32).astype(ml_dtypes.bfloat16).astype(np.float64), axis, -1)
    blocks = v.reshape(v.shape[:-1] + (-1, 32))
    amax = np.abs(blocks).max(-1, keepdims=True)
    byte = np.maximum(np.where(amax > 0, np.frexp(amax)[1] - 1 + 127, 0) - down, 1)
    scale = np.exp2(byte - 127.0)
    codes = (blocks / scale).astype(np.float32).astype(dtype).astype(np.float64)
    return np.moveaxis((codes * scale).reshape(v.shape), -1, axis)


WIDE = False


def mx_kscale(k):
    if not WIDE:
        return np.ones(k)
    levels = np.array([10, -10, 5, -5, 0])
    if k % 512:
        return np.exp2(np.random.permutation(np.resize(levels, k // 32))).repeat(32)
    a = np.empty((k // 512, 16))
    for p in range(k // 512):
        a[p, :8] = np.random.permutation(np.resize(levels, 8))
        for g in range(8):
            far = levels[np.abs(levels - a[p, g]) >= 10]
            a[p, g + 8] = far[np.random.randint(len(far))]
    return np.exp2(a.ravel()).repeat(32)


BF16 = ml_dtypes.bfloat16


def bf(x):
    return np.asarray(x, np.float32).astype(BF16)


def f64(x):
    return np.asarray(x).astype(np.float64)


E2M1 = np.array([0.0, 0.5, 1.0, 1.5, 2.0, 3.0, 4.0, 6.0, -0.0, -0.5, -1.0, -1.5, -2.0, -3.0, -4.0, -6.0])


def pack_weight(w, fmt):
    k, n = w.shape
    w = f64(bf(w)).reshape(k // 32, 32, n)
    amax = np.abs(w).max(1)
    if fmt == "e4m3":
        byte = np.frexp(amax)[1] - 1 + 127 - 7
    else:
        mant, ex = np.frexp(amax / 6.0)
        byte = np.where(mant > 0.5, ex, ex - 1) + 127
    byte = np.clip(np.where(amax > 0, byte, 1), 1, 254)
    scaled = (w * np.exp2(127.0 - byte)[:, None, :]).reshape(k, n).astype(np.float32)
    by_word = np.ascontiguousarray(scaled.reshape(k // 512, 128, 4, n).transpose(0, 1, 3, 2))
    if fmt == "e4m3":
        words = by_word.astype(ml_dtypes.float8_e4m3fn).view(np.uint8)
    else:
        c = by_word.astype(ml_dtypes.float4_e2m1fn).view(np.uint8) & 0xF
        words = c[..., 0::2] | (c[..., 1::2] << 4)
    return np.ascontiguousarray(words), np.ascontiguousarray(byte.astype(np.uint8).reshape(k // 512, 16, n))


def unpack_weight(words, scales, fmt):
    g, p, n, _ = words.shape
    if fmt == "e4m3":
        vals = np.ascontiguousarray(words).view(ml_dtypes.float8_e4m3fn).astype(np.float64)
    else:
        nib = np.empty((g, p, n, 4), np.uint8)
        nib[..., 0::2] = words & 0xF
        nib[..., 1::2] = words >> 4
        vals = E2M1[nib]
    vals = vals * np.repeat(np.exp2(scales.astype(np.float64) - 127.0), 8, axis=1)[..., None]
    return vals.transpose(0, 1, 3, 2).reshape(g * 512, n)
def pack4(w):
    words, scales = pack_weight(w, "e2m1")
    return words.reshape(words.shape[0], 128, -1), scales


def unpack4(words, scales):
    return unpack_weight(words.reshape(words.shape[0], 128, -1, 2), scales, "e2m1")


T, C, D, E, H = 2048, 4, 1024, 1024, 512


def sigmoid(a):
    return 1.0 / (1.0 + np.exp(-a))


def draw0():
    s, v = mx_kscale(D), mx_kscale(E)
    x = bf(np.random.standard_normal((T, D)) * s)
    wv_words, wv_scales = pack4(np.random.standard_normal((D, E)) / np.sqrt(D) / s[:, None])
    wz_words, wz_scales = pack4(np.random.standard_normal((D, E)) / np.sqrt(D) / s[:, None])
    pos = bf(0.5 * np.random.standard_normal((C, E)))
    gain = bf((1.0 + 0.1 * np.random.standard_normal(E)) * v)
    wu_words, wu_scales = pack4(np.random.standard_normal((E, H)) / np.sqrt(E) / v[:, None])
    wr_words, wr_scales = pack4(np.random.standard_normal((E, H)) / np.sqrt(E) / v[:, None])
    bu = bf(0.3 * np.random.standard_normal(H))
    br = bf(0.5 * np.random.standard_normal(H))
    mem = bf(np.random.standard_normal((T // C, H)))
    return {"x": x, "wv_words": wv_words, "wv_scales": wv_scales,
            "wz_words": wz_words, "wz_scales": wz_scales, "pos": pos, "gain": gain,
            "wu_words": wu_words, "wu_scales": wu_scales,
            "wr_words": wr_words, "wr_scales": wr_scales,
            "bu": bu, "br": br, "mem": mem}


def core(x, wv_words, wv_scales, wz_words, wz_scales, pos, gain,
              wu_words, wu_scales, wr_words, wr_scales, bu, br, mem):
    xq = mxq(f64(x), 1, "e4m3")
    val = xq @ unpack4(wv_words, wv_scales)
    log = xq @ unpack4(wz_words, wz_scales)
    val = val.reshape(T // C, C, E)
    log = log.reshape(T // C, C, E) + f64(pos)[None, :, :]
    e = np.exp(log - log.max(axis=1, keepdims=True))
    pooled = (e * val).sum(axis=1) / e.sum(axis=1)
    c = pooled / np.sqrt((pooled * pooled).mean(axis=1, keepdims=True)) * f64(gain)[None, :]
    cq = mxq(c, 1, "e4m3")
    u = (cq @ unpack4(wu_words, wu_scales)) + f64(bu)[None, :]
    r = sigmoid((cq @ unpack4(wr_words, wr_scales)) + f64(br)[None, :])
    return r * f64(mem) + (1.0 - r) * u


def e4m3fn_bytes(y):
    return np.clip(np.asarray(y, np.float64), -448.0, 448.0).astype(np.float32).astype(ml_dtypes.float8_e4m3fn).view(np.uint8)


def e4m3fn_values(b):
    return np.asarray(b, np.uint8).view(ml_dtypes.float8_e4m3fn).astype(np.float64)


def setup_inputs():
    d = draw0()
    x0 = np.asarray(d['x']).astype(np.float64)
    s = (np.max(np.abs(x0), axis=(0,), keepdims=True) / 448.0).astype(np.float32)
    out = {}
    for k, v in d.items():
        if k == 'x':
            out['x_bytes'] = e4m3fn_bytes(x0 / s.astype(np.float64))
            out['x_scale'] = s
        else:
            out[k] = v
    return out


def reference(x_bytes, x_scale, wv_words, wv_scales, wz_words, wz_scales, pos, gain, wu_words, wu_scales, wr_words, wr_scales, bu, br, mem):
    return core(e4m3fn_values(x_bytes) * x_scale.astype(np.float64), wv_words, wv_scales, wz_words, wz_scales, pos, gain, wu_words, wu_scales, wr_words, wr_scales, bu, br, mem)

@@ -1,0 +1,449 @@
+from contextlib import ExitStack
+
+import concourse.mybir as mybir
+from concourse.masks import make_identity
+
+F32 = mybir.dt.float32
+BF16 = mybir.dt.bfloat16
+I32 = mybir.dt.int32
+U32 = mybir.dt.uint32
+U8 = mybir.dt.uint8
+FP8 = mybir.dt.float8_e4m3fn
+FP8X4 = mybir.dt.float8_e4m3fn_x4
+FP4X4 = mybir.dt.float4_e2m1fn_x4
+AF = mybir.ActivationFunctionType
+ALU = mybir.AluOpType
+
+T, C, D, E, H = 2048, 4, 1024, 1024, 512
+SLOTS = T // C
+P = 128
+G = D // 512
+NB = SLOTS // P
+TOK = C * P
+NCH = E // P
+PAIRS = NB * NCH // 2
+
+BANKS = {"z": 2, "a": 4, "nd": 1, "xt": 1}
+
+FLOPS = 2 * T * D * 2 * E + 2 * SLOTS * E * 2 * H
+
+
+def tile_compressive_memory_update_f1_kernel(
+    tc, x_bytes, x_scale, wv_words, wv_scales, wz_words, wz_scales, pos, gain,
+    wu_words, wu_scales, wr_words, wr_scales, bu, br, mem, out,
+):
+    nc = tc.nc
+    with ExitStack() as ctx:
+        sb = ctx.enter_context(tc.tile_pool(name="sb", bufs=1))
+        ps = ctx.enter_context(tc.psum_pool(name="ps", bufs=2))
+        ctx.enter_context(tc.manual_schedule())
+
+        def keep(shape, dtype, name):
+            return sb.tile(shape, dtype, name=name, tag=name, bufs=1, align_bytes=64)
+
+        def cycle(shape, dtype, name, bufs):
+            return sb.tile(shape, dtype, name=name, tag=name, bufs=bufs, align_bytes=64)
+
+        def bank(shape, dtype, name):
+            return ps.tile(shape, dtype, name=name, tag=name, bufs=BANKS[name])
+
+        xv = x_bytes.rearrange("(b j i) k -> b j i k", j=P, i=C)
+        xb = []
+        for b in range(NB):
+            t = keep([P, C, D], U8, "xb%d" % b)
+            xb.append(t)
+        xs = keep([P, D], F32, "xs")
+        xsv = x_scale.rearrange("o k -> (o k)")
+        for h in range(2):
+            cols = slice(512 * h, 512 * (h + 1))
+            nc.scalar.dma_start(out=xs[:, cols], in_=xsv[cols].partition_broadcast(P))
+        for i in range(C):
+            nc.sync.dma_start(out=xb[0][:, i, :], in_=xv[0][:, i, :])
+
+        pos_rows = keep([P, P], BF16, "pos_rows")
+        nc.vector.memset(pos_rows[:], 0.0)
+        nc.scalar.dma_start(out=pos_rows[0 : C * NCH, :], in_=pos.rearrange("i (c p) -> (i c) p", p=P))
+
+        dummy = keep([P, 1], F32, "dummy")
+        nc.vector.memset(dummy[:], 0.0)
+        nc.scalar.activation(out=dummy[:], in_=dummy[:], func=AF.Exp)
+
+        def load_weight(name, n):
+            w = keep([P, G, 2 * n], U8, name)
+            plane = keep([P, G, n], U8, name + "_s")
+            nc.gpsimd.memset(plane[:].rearrange("p g n -> p (g n)").bitcast(I32), 0)
+            return w, plane
+
+        def fetch_scales(plane, scales):
+            for q in range(4):
+                nc.sync.dma_start(
+                    out=plane[32 * q : 32 * q + 4, :, :].bitcast(I32),
+                    in_=scales[:, 4 * q : 4 * q + 4, :].rearrange("g q n -> q g n").bitcast(I32),
+                )
+
+        def fetch_words(w, words):
+            nc.sync.dma_start(out=w[:], in_=words.rearrange("g p n -> p g n"))
+
+        wz, wzs = load_weight("wz", E)
+        wv, wvs = load_weight("wv", E)
+        ident = keep([P, P], F32, "ident")
+        make_identity(nc, ident[:])
+        identb = keep([P, P], BF16, "identb")
+        make_identity(nc, identb[:])
+        wu, wus = load_weight("wu", H)
+        wr, wrs = load_weight("wr", H)
+        half = keep([P, 1], F32, "half")
+        nc.gpsimd.memset(half[:], -0.5)
+
+        fetch_scales(wzs, wz_scales)
+        fetch_scales(wvs, wv_scales)
+        nc.sync.dma_start(out=xb[1][:], in_=xv[1])
+        fetch_words(wz, wz_words)
+        fetch_words(wv, wv_words)
+        nc.sync.dma_start(out=xb[2][:], in_=xv[2])
+        nc.sync.dma_start(out=xb[3][:], in_=xv[3])
+        fetch_scales(wus, wu_scales)
+        fetch_scales(wrs, wr_scales)
+        fetch_words(wu, wu_words)
+        fetch_words(wr, wr_words)
+        memt = keep([P, NB, H], BF16, "memt")
+        nc.sync.dma_start(out=memt[:], in_=mem.rearrange("(b j) h -> j b h", j=P))
+        bub = keep([P, H], BF16, "bub")
+        nc.sync.dma_start(out=bub[:], in_=bu.partition_broadcast(P))
+        brb = keep([P, H], BF16, "brb")
+        nc.sync.dma_start(out=brb[:], in_=br.partition_broadcast(P))
+        gainb = keep([P, E], BF16, "gainb")
+        nc.sync.dma_start(out=gainb[:], in_=gain.partition_broadcast(P))
+        mb = keep([P, NB, H], F32, "mb")
+
+        xw, xg, xq, xqs, xt = {}, {}, {}, {}, {}
+
+        def x_product(b, i, halves=1):
+            t = cycle([P, D], BF16, "xw", 3)
+            n = D // halves
+            for h in range(halves):
+                cols = slice(n * h, n * (h + 1))
+                nc.vector.tensor_tensor(
+                    out=t[:, cols], in0=xb[b][:, i, cols].bitcast(FP8), in1=xs[:, cols], op=ALU.mult
+                )
+            xw[b, i] = t
+
+        def turn(src, dst):
+            words = src[:].bitcast(F32)
+            for g in range(G):
+                for u in range(2):
+                    nc.tensor.transpose(dst[:, g, u, :], words[:, 256 * g + u : 256 * (g + 1) : 2], ident[:])
+
+        def x_turn(b, i, name="xt"):
+            if i == 0:
+                xg[b] = cycle([P, G, TOK, 2], F32, "xg", 2)
+                xq[b] = cycle([P, G, TOK], U32, "xq", 2)
+                xqs[b] = cycle([P, G, TOK], U8, "xqs", 2)
+            xt[b, i] = bank([P, G, 2, P], F32, name)
+            turn(xw[b, i], xt[b, i])
+
+        def x_evac(b, i):
+            nc.scalar.copy(
+                out=xg[b][:, :, P * i : P * (i + 1), :], in_=xt[b, i][:].rearrange("p g u j -> p g j u")
+            )
+
+        def x_quant(b, i0, i1):
+            cols = slice(P * i0, P * i1)
+            for g in range(G):
+                nc.vector.quantize_mx(
+                    out=xq[b][:, g, cols].bitcast(FP8X4),
+                    scales=xqs[b][:, g, cols],
+                    in_=xg[b][:, g, cols, :].rearrange("p n u -> p (n u)").bitcast(BF16),
+                )
+
+        z, a, lg, mx1, mx, dd, ee, pr, nd, num, den2 = {}, {}, {}, {}, {}, {}, {}, {}, {}, {}, {}
+
+        def project(q, w, ws, name, dst):
+            for v in range(2):
+                s = 2 * q + v
+                b, c = divmod(s, NCH)
+                dst[s] = bank([P, C, P], F32, name)
+                for g in range(G):
+                    nc.tensor.matmul_mx(
+                        out=dst[s][:].rearrange("p i j -> p (i j)"),
+                        lhsT=w[:, g, 2 * P * c : 2 * P * (c + 1)].bitcast(FP4X4),
+                        lhsT_scale=ws[:, g, P * c : P * (c + 1)],
+                        rhs=xq[b][:, g, :].bitcast(FP8X4),
+                        rhs_scale=xqs[b][:, g, :],
+                        start=(g == 0),
+                        stop=(g == G - 1),
+                    )
+
+        pos_bank = bank([P, P], BF16, "xt")
+        nc.tensor.transpose(pos_bank[:], pos_rows[:], identb[:])
+        pos_col = keep([P, C * NCH], F32, "pos_col")
+        nc.scalar.copy(out=pos_col[:], in_=pos_bank[:, 0 : C * NCH])
+
+        def logits(q):
+            lg[q] = cycle([P, 2, C, P], F32, "lg", 3)
+            for v in range(2):
+                s = 2 * q + v
+                for i in range(C):
+                    k = i * NCH + s % NCH
+                    nc.scalar.activation(
+                        out=lg[q][:, v, i, :], in_=z[s][:, i, :], func=AF.Identity,
+                        bias=pos_col[:, k : k + 1], scale=1.0,
+                    )
+
+        def max_a(q):
+            t = cycle([P, 2, 2, P], F32, "mx1", 2)
+            nc.vector.tensor_tensor(
+                out=t[:], in0=lg[q][:, :, 0:2, :], in1=lg[q][:, :, 2:4, :], op=ALU.max
+            )
+            mx1[q] = t
+
+        def max_b(q):
+            t = cycle([P, 2, P], F32, "mx", 2)
+            nc.vector.tensor_tensor(out=t[:], in0=mx1[q][:, :, 0, :], in1=mx1[q][:, :, 1, :], op=ALU.max)
+            mx[q] = t
+
+        def subtract(q, v, eng):
+            if q not in dd:
+                dd[q] = cycle([P, 2, C, P], F32, "dd", 2)
+            eng.tensor_tensor(
+                out=dd[q][:, v, :, :], in0=lg[q][:, v, :, :],
+                in1=mx[q][:, v, :].unsqueeze(1).to_broadcast([P, C, P]), op=ALU.subtract,
+            )
+
+        def expo(q):
+            t = cycle([P, 2, C, P], F32, "ee", 3)
+            nc.scalar.activation(out=t[:], in_=dd[q][:], func=AF.Exp)
+            ee[q] = t
+
+        def weigh(q):
+            t = cycle([P, 2, C, P], F32, "pr", 2)
+            for v in range(2):
+                nc.vector.tensor_tensor(out=t[:, v, :, :], in0=ee[q][:, v, :, :], in1=a[2 * q + v][:], op=ALU.mult)
+            pr[q] = t
+
+        def sums(q):
+            b = q // (NCH // 2)
+            if q % (NCH // 2) == 0:
+                num[b] = keep([P, E], F32, "num%d" % b)
+                den2[b] = keep([P, E], F32, "den%d" % b)
+            t = bank([P, 2, 2, P], F32, "nd")
+            for k, src in ((0, pr[q]), (1, ee[q])):
+                for v in range(2):
+                    for i in range(C):
+                        nc.tensor.matmul(
+                            out=t[:, k, v, :], lhsT=src[:, v, i, :], rhs=ident[:],
+                            start=(i == 0), stop=(i == C - 1), is_transpose=True,
+                        )
+            nd[q] = t
+
+        def sums_out(q):
+            b, c = divmod(q, NCH // 2)
+            cols = slice(2 * P * c, 2 * P * (c + 1))
+            nc.scalar.copy(out=num[b][:, cols], in_=nd[q][:, 0, :, :].rearrange("p v n -> p (v n)"))
+            nc.scalar.activation(
+                out=den2[b][:, cols], in_=nd[q][:, 1, :, :].rearrange("p v n -> p (v n)"), func=AF.Square
+            )
+
+        yy, yt, yg, yq, yqs, uu, rr, ssq, rsd, gate, diff, frac = {}, {}, {}, {}, {}, {}, {}, {}, {}, {}, {}, {}
+
+        def less_bias(b, eng):
+            eng.tensor_tensor(out=mb[:, b, :], in0=memt[:, b, :], in1=bub[:], op=ALU.subtract)
+
+        def recip(b):
+            nc.scalar.activation(out=den2[b][:], in_=den2[b][:], func=AF.Abs_reciprocal_sqrt)
+
+        def pooled(b):
+            nc.vector.tensor_tensor(out=num[b][:], in0=num[b][:], in1=den2[b][:], op=ALU.mult)
+
+        def square(b):
+            junk = cycle([P, E], BF16, "junk", 1)
+            ssq[b] = keep([P, 1], F32, "ssq%d" % b)
+            nc.scalar.activation(
+                out=junk[:], in_=num[b][:], func=AF.Square, scale=1.0 / 32.0, accum_out=ssq[b][:]
+            )
+
+        def root(b):
+            rsd[b] = keep([P, 1], F32, "rsd%d" % b)
+            nc.gpsimd.tensor_tensor(out=rsd[b][:], in0=ssq[b][:], in1=half[:], op=ALU.pow)
+
+        def norm(b):
+            yy[b] = cycle([P, E], BF16, "yy", 2)
+            nc.vector.scalar_tensor_tensor(
+                out=yy[b][:], in0=num[b][:], scalar=rsd[b][:], in1=gainb[:], op0=ALU.mult, op1=ALU.mult
+            )
+
+        def y_turn(b, name):
+            yt[b] = bank([P, G, 2, P], F32, name)
+            turn(yy[b], yt[b])
+
+        def y_evac(b, copy):
+            yg[b] = cycle([P, G, P, 2], F32, "yg", 2)
+            copy(out=yg[b][:], in_=yt[b][:].rearrange("p g u j -> p g j u"))
+
+        def y_quant(b):
+            yq[b] = cycle([P, G * P], U32, "yq", 3)
+            yqs[b] = cycle([P, G * P], U8, "yqs", 3)
+            nc.vector.quantize_mx(
+                out=yq[b][:].bitcast(FP8X4), scales=yqs[b][:],
+                in_=yg[b][:].rearrange("p g n u -> p (g n u)").bitcast(BF16),
+            )
+
+        def second(b, w, ws, name, dst):
+            dst[b] = bank([P, H], F32, name)
+            for g in range(G):
+                cols = slice(P * g, P * (g + 1))
+                nc.tensor.matmul_mx(
+                    out=dst[b][:], lhsT=yq[b][:, cols].bitcast(FP8X4), lhsT_scale=yqs[b][:, cols],
+                    rhs=w[:, g, :].bitcast(FP4X4), rhs_scale=ws[:, g, :],
+                    start=(g == 0), stop=(g == G - 1),
+                )
+
+        def gate_in(b):
+            gate[b] = cycle([P, H], F32, "gate", 4)
+            nc.vector.tensor_tensor(out=gate[b][:], in0=rr[b][:], in1=brb[:], op=ALU.add)
+
+        def gate_out(b):
+            nc.scalar.activation(out=gate[b][:], in_=gate[b][:], func=AF.Sigmoid, scale=-1.0)
+
+        def difference(b):
+            diff[b] = cycle([P, H], F32, "diff", 4)
+            nc.vector.tensor_tensor(out=diff[b][:], in0=uu[b][:], in1=mb[:, b, :], op=ALU.subtract)
+
+        def mix(b, eng):
+            eng.tensor_tensor(out=diff[b][:], in0=gate[b][:], in1=diff[b][:], op=ALU.mult)
+
+        def store(b, eng):
+            o = cycle([P, H], F32, "o", 4)
+            eng.tensor_tensor(out=o[:], in0=diff[b][:], in1=memt[:, b, :], op=ALU.add)
+            nc.sync.dma_start(out=out[P * b : P * (b + 1), :], in_=o[:])
+
+        names = ("a", "a", "nd", "xt")
+        for i in range(C):
+            x_product(0, i, 2)
+            x_turn(0, i, names[i])
+            x_evac(0, i)
+            if i == 2:
+                x_quant(0, 0, 2)
+        x_product(1, 0)
+        x_quant(0, 2, 4)
+        project(0, wz, wzs, "z", z)
+        project(0, wv, wvs, "a", a)
+        logits(0)
+        x_product(1, 1)
+        x_turn(1, 0)
+        x_evac(1, 0)
+        x_product(1, 2)
+        x_turn(1, 1)
+        x_evac(1, 1)
+
+        for q in range(PAIRS + 1):
+            live = q < PAIRS
+            made, turned = q + 3, q + 2
+            last = C * (NB - 1)
+
+            def mx_work():
+                if q + 1 < PAIRS:
+                    project(q + 1, wz, wzs, "z", z)
+                if live and q > 0:
+                    project(q, wv, wvs, "a", a)
+
+            def turn_work():
+                if 0 <= q - 2 < PAIRS:
+                    sums(q - 2)
+                if turned < last:
+                    x_turn(turned // C + 1, turned % C)
+
+            if live:
+                max_a(q)
+            if 0 <= q - 1 < PAIRS:
+                expo(q - 1)
+            if made < last:
+                x_product(made // C + 1, made % C)
+            if q % 2 == 0:
+                mx_work()
+                turn_work()
+            else:
+                turn_work()
+                mx_work()
+            if live:
+                max_b(q)
+                subtract(q, 1, nc.gpsimd)
+            if q + 1 < PAIRS:
+                logits(q + 1)
+            if 0 <= q - 1 < PAIRS:
+                weigh(q - 1)
+            if live:
+                subtract(q, 0, nc.vector)
+            if q % C == 2 and q // C + 1 < NB:
+                x_quant(q // C + 1, 0, C)
+            if 0 <= q - 2 < PAIRS:
+                sums_out(q - 2)
+            if turned < last:
+                x_evac(turned // C + 1, turned % C)
+
+        sums(PAIRS - 1)
+        recip(1)
+        less_bias(0, nc.vector)
+        less_bias(1, nc.vector)
+        less_bias(2, nc.vector)
+        less_bias(3, nc.vector)
+        recip(0)
+        sums_out(PAIRS - 1)
+        pooled(1)
+        recip(3)
+        pooled(0)
+        pooled(3)
+        square(0)
+        square(1)
+        root(0)
+        norm(0)
+        square(3)
+        root(1)
+        norm(1)
+        y_turn(0, "nd")
+        root(3)
+        norm(3)
+        recip(2)
+        pooled(2)
+        y_turn(3, "xt")
+        y_evac(0, nc.scalar.copy)
+        y_quant(0)
+        square(2)
+        y_evac(3, nc.vector.tensor_copy)
+        y_turn(1, "nd")
+        y_quant(3)
+        y_evac(1, nc.scalar.copy)
+        second(0, wr, wrs, "z", rr)
+        gate_in(0)
+        second(0, wu, wus, "a", uu)
+        gate_out(0)
+        y_quant(1)
+        root(2)
+        norm(2)
+        second(3, wr, wrs, "z", rr)
+        second(1, wu, wus, "a", uu)
+        difference(1)
+        second(1, wr, wrs, "z", rr)
+        y_turn(2, "xt")
+        y_evac(2, nc.scalar.copy)
+        gate_in(1)
+        difference(0)
+        gate_out(1)
+        y_quant(2)
+        second(3, wu, wus, "a", uu)
+        second(2, wu, wus, "a", uu)
+        mix(0, nc.gpsimd)
+        gate_in(3)
+        second(2, wr, wrs, "z", rr)
+        difference(3)
+        store(0, nc.gpsimd)
+        gate_out(3)
+        difference(2)
+        gate_in(2)
+        gate_out(2)
+        mix(1, nc.gpsimd)
+        mix(3, nc.vector)
+        store(3, nc.vector)
+        store(1, nc.gpsimd)
+        mix(2, nc.vector)
+        store(2, nc.vector)

@@ -202,24 +202,25 @@ def tile_compressive_memory_update_f1_kernel(
             nc.vector.tensor_tensor(out=t[:], in0=mx1[q][:, :, 0, :], in1=mx1[q][:, :, 1, :], op=ALU.max)
             mx[q] = t
 
-        def subtract(q, v, eng):
+        def subtract(q, v0, v1, eng):
             if q not in dd:
                 dd[q] = cycle([P, 2, C, P], F32, "dd", 2)
             eng.tensor_tensor(
-                out=dd[q][:, v, :, :], in0=lg[q][:, v, :, :],
-                in1=mx[q][:, v, :].unsqueeze(1).to_broadcast([P, C, P]), op=ALU.subtract,
+                out=dd[q][:, v0:v1, :, :], in0=lg[q][:, v0:v1, :, :],
+                in1=mx[q][:, v0:v1, :].unsqueeze(2).to_broadcast([P, v1 - v0, C, P]), op=ALU.subtract,
             )
 
-        def expo(q):
-            t = cycle([P, 2, C, P], F32, "ee", 3)
-            nc.scalar.activation(out=t[:], in_=dd[q][:], func=AF.Exp)
-            ee[q] = t
+        def expo(q, v):
+            if v == 0:
+                ee[q] = cycle([P, 2, C, P], F32, "ee", 3)
+            nc.scalar.activation(out=ee[q][:, v, :, :], in_=dd[q][:, v, :, :], func=AF.Exp)
 
-        def weigh(q):
-            t = cycle([P, 2, C, P], F32, "pr", 2)
-            for v in range(2):
-                nc.vector.tensor_tensor(out=t[:, v, :, :], in0=ee[q][:, v, :, :], in1=a[2 * q + v][:], op=ALU.mult)
-            pr[q] = t
+        def weigh(q, v):
+            if v == 0:
+                pr[q] = cycle([P, 2, C, P], F32, "pr", 2)
+            nc.vector.tensor_tensor(
+                out=pr[q][:, v, :, :], in0=ee[q][:, v, :, :], in1=a[2 * q + v][:], op=ALU.mult
+            )
 
         def sums(q):
             b = q // (NCH // 2)
@@ -341,39 +342,33 @@ def tile_compressive_memory_update_f1_kernel(
             made, turned = q + 3, q + 2
             last = C * (NB - 1)
 
-            def mx_work():
-                if q + 1 < PAIRS:
-                    project(q + 1, wz, wzs, "z", z)
-                if live and q > 0:
-                    project(q, wv, wvs, "a", a)
-
-            def turn_work():
-                if 0 <= q - 2 < PAIRS:
-                    sums(q - 2)
-                if turned < last:
-                    x_turn(turned // C + 1, turned % C)
-
+            if q + 1 < PAIRS:
+                project(q + 1, wz, wzs, "z", z)
             if live:
                 max_a(q)
             if 0 <= q - 1 < PAIRS:
-                expo(q - 1)
-            if made < last:
-                x_product(made // C + 1, made % C)
-            if q % 2 == 0:
-                mx_work()
-                turn_work()
-            else:
-                turn_work()
-                mx_work()
+                weigh(q - 1, 0)
+            if live and q > 0:
+                project(q, wv, wvs, "a", a)
+            if 0 <= q - 2 < PAIRS:
+                sums(q - 2)
+            if turned < last:
+                x_turn(turned // C + 1, turned % C)
             if live:
                 max_b(q)
-                subtract(q, 1, nc.gpsimd)
+            if made < last:
+                x_product(made // C + 1, made % C)
             if q + 1 < PAIRS:
                 logits(q + 1)
-            if 0 <= q - 1 < PAIRS:
-                weigh(q - 1)
+            if made >= last and 0 <= q - 1 < PAIRS:
+                weigh(q - 1, 1)
             if live:
-                subtract(q, 0, nc.vector)
+                subtract(q, 0, 2, nc.vector)
+                expo(q, 0)
+                expo(q, 1)
+            if made < last:
+                if q > 0:
+                    weigh(q - 1, 1)
             if q % C == 2 and q // C + 1 < NB:
                 x_quant(q // C + 1, 0, C)
             if 0 <= q - 2 < PAIRS:

@@ -52,11 +52,10 @@ def tile_compressive_memory_update_f1_kernel(
         for b in range(NB):
             t = keep([P, C, D], U8, "xb%d" % b)
             xb.append(t)
-        xs = keep([P, D], F32, "xs")
-        xsv = x_scale.rearrange("o k -> (o k)")
-        for h in range(2):
-            cols = slice(512 * h, 512 * (h + 1))
-            nc.scalar.dma_start(out=xs[:, cols], in_=xsv[cols].partition_broadcast(P))
+        xs_col = keep([P, G, 8], F32, "xs_col")
+        nc.scalar.dma_start(
+            out=xs_col[:, :, 0:4], in_=x_scale.rearrange("o (g p t) -> p (o g) t", p=P, t=4)
+        )
         for i in range(C):
             nc.sync.dma_start(out=xb[0][:, i, :], in_=xv[0][:, i, :])
 
@@ -84,10 +83,10 @@ def tile_compressive_memory_update_f1_kernel(
         def fetch_words(w, words):
             nc.sync.dma_start(out=w[:], in_=words.rearrange("g p n -> p g n"))
 
-        wz, wzs = load_weight("wz", E)
-        wv, wvs = load_weight("wv", E)
         ident = keep([P, P], F32, "ident")
         make_identity(nc, ident[:])
+        wz, wzs = load_weight("wz", E)
+        wv, wvs = load_weight("wv", E)
         identb = keep([P, P], BF16, "identb")
         make_identity(nc, identb[:])
         wu, wus = load_weight("wu", H)
@@ -96,10 +95,10 @@ def tile_compressive_memory_update_f1_kernel(
         nc.gpsimd.memset(half[:], -0.5)
 
         fetch_scales(wzs, wz_scales)
-        fetch_scales(wvs, wv_scales)
-        nc.sync.dma_start(out=xb[1][:], in_=xv[1])
         fetch_words(wz, wz_words)
+        fetch_scales(wvs, wv_scales)
         fetch_words(wv, wv_words)
+        nc.sync.dma_start(out=xb[1][:], in_=xv[1])
         nc.sync.dma_start(out=xb[2][:], in_=xv[2])
         nc.sync.dma_start(out=xb[3][:], in_=xv[3])
         fetch_scales(wus, wu_scales)
@@ -115,6 +114,16 @@ def tile_compressive_memory_update_f1_kernel(
         gainb = keep([P, E], BF16, "gainb")
         nc.sync.dma_start(out=gainb[:], in_=gain.partition_broadcast(P))
         mb = keep([P, NB, H], F32, "mb")
+
+        xs = keep([P, D], F32, "xs")
+        for g in range(G):
+            t = bank([P, 4, P], F32, "z")
+            for k in range(4):
+                nc.tensor.transpose(t[:, k, :], xs_col[:, g, k : k + 1].to_broadcast([P, P]), ident[:])
+            nc.scalar.copy(
+                out=xs[:, 512 * g : 512 * (g + 1)].rearrange("p (n t) -> p n t", t=4),
+                in_=t[:].rearrange("p t n -> p n t"),
+            )
 
         xw, xg, xq, xqs, xt = {}, {}, {}, {}, {}
 
@@ -174,16 +183,33 @@ def tile_compressive_memory_update_f1_kernel(
                         stop=(g == G - 1),
                     )
 
+        def project_tile(w, ws, name, dst, i):
+            for v in range(2):
+                if i == 0:
+                    dst[v] = bank([P, C, P], F32, name)
+                cols = slice(P * i, P * (i + 1))
+                for g in range(G):
+                    nc.tensor.matmul_mx(
+                        out=dst[v][:, i, :],
+                        lhsT=w[:, g, 2 * P * v : 2 * P * (v + 1)].bitcast(FP4X4),
+                        lhsT_scale=ws[:, g, P * v : P * (v + 1)],
+                        rhs=xq[0][:, g, cols].bitcast(FP8X4),
+                        rhs_scale=xqs[0][:, g, cols],
+                        start=(g == 0),
+                        stop=(g == G - 1),
+                    )
+
         pos_bank = bank([P, P], BF16, "xt")
         nc.tensor.transpose(pos_bank[:], pos_rows[:], identb[:])
         pos_col = keep([P, C * NCH], F32, "pos_col")
         nc.scalar.copy(out=pos_col[:], in_=pos_bank[:, 0 : C * NCH])
 
-        def logits(q):
-            lg[q] = cycle([P, 2, C, P], F32, "lg", 3)
+        def logits(q, i0=0, i1=C):
+            if i0 == 0:
+                lg[q] = cycle([P, 2, C, P], F32, "lg", 3)
             for v in range(2):
                 s = 2 * q + v
-                for i in range(C):
+                for i in range(i0, i1):
                     k = i * NCH + s % NCH
                     nc.scalar.activation(
                         out=lg[q][:, v, i, :], in_=z[s][:, i, :], func=AF.Identity,
@@ -222,20 +248,24 @@ def tile_compressive_memory_update_f1_kernel(
                 out=pr[q][:, v, :, :], in0=ee[q][:, v, :, :], in1=a[2 * q + v][:], op=ALU.mult
             )
 
-        def sums(q):
+        def sums(q, k=None):
+            if k is None:
+                sums(q, 0)
+                sums(q, 1)
+                return
             b = q // (NCH // 2)
-            if q % (NCH // 2) == 0:
-                num[b] = keep([P, E], F32, "num%d" % b)
-                den2[b] = keep([P, E], F32, "den%d" % b)
-            t = bank([P, 2, 2, P], F32, "nd")
-            for k, src in ((0, pr[q]), (1, ee[q])):
-                for v in range(2):
-                    for i in range(C):
-                        nc.tensor.matmul(
-                            out=t[:, k, v, :], lhsT=src[:, v, i, :], rhs=ident[:],
-                            start=(i == 0), stop=(i == C - 1), is_transpose=True,
-                        )
-            nd[q] = t
+            if k == 0:
+                nd[q] = bank([P, 2, 2, P], F32, "nd")
+                if q % (NCH // 2) == 0:
+                    num[b] = keep([P, E], F32, "num%d" % b)
+                    den2[b] = keep([P, E], F32, "den%d" % b)
+            src = (pr[q], ee[q])[k]
+            for v in range(2):
+                for i in range(C):
+                    nc.tensor.matmul(
+                        out=nd[q][:, k, v, :], lhsT=src[:, v, i, :], rhs=ident[:],
+                        start=(i == 0), stop=(i == C - 1), is_transpose=True,
+                    )
 
         def sums_out(q):
             b, c = divmod(q, NCH // 2)
@@ -319,17 +349,25 @@ def tile_compressive_memory_update_f1_kernel(
             nc.sync.dma_start(out=out[P * b : P * (b + 1), :], in_=o[:])
 
         names = ("a", "a", "nd", "xt")
+
+        def begin(i, w, ws, name, dst):
+            project_tile(w, ws, name, dst, i)
+
         for i in range(C):
             x_product(0, i, 2)
+            if i > 0:
+                x_quant(0, i - 1, i)
             x_turn(0, i, names[i])
             x_evac(0, i)
-            if i == 2:
-                x_quant(0, 0, 2)
+            if i > 1:
+                begin(i - 2, wz, wzs, "z", z)
+                logits(0, i - 2, i - 1)
         x_product(1, 0)
-        x_quant(0, 2, 4)
-        project(0, wz, wzs, "z", z)
+        x_quant(0, 3, 4)
+        for i in (2, 3):
+            begin(i, wz, wzs, "z", z)
+            logits(0, i, i + 1)
         project(0, wv, wvs, "a", a)
-        logits(0)
         x_product(1, 1)
         x_turn(1, 0)
         x_evac(1, 0)

@@ -128,7 +128,7 @@ def tile_compressive_memory_update_f1_kernel(
         xw, xg, xq, xqs, xt = {}, {}, {}, {}, {}
 
         def x_product(b, i, halves=1):
-            t = cycle([P, D], BF16, "xw", 3)
+            t = cycle([P, D], BF16, "xw", 4)
             n = D // halves
             for h in range(halves):
                 cols = slice(n * h, n * (h + 1))
@@ -237,7 +237,7 @@ def tile_compressive_memory_update_f1_kernel(
             )
 
         def expo(q, v):
-            if v == 0:
+            if q not in ee:
                 ee[q] = cycle([P, 2, C, P], F32, "ee", 3)
             nc.scalar.activation(out=ee[q][:, v, :, :], in_=dd[q][:, v, :, :], func=AF.Exp)
 
@@ -375,16 +375,19 @@ def tile_compressive_memory_update_f1_kernel(
         x_turn(1, 1)
         x_evac(1, 1)
 
-        for q in range(PAIRS + 1):
+        for q in range(PAIRS):
             live = q < PAIRS
             made, turned = q + 3, q + 2
             last = C * (NB - 1)
 
             if q + 1 < PAIRS:
                 project(q + 1, wz, wzs, "z", z)
+            ending = q == PAIRS - 1
             if live:
                 max_a(q)
-            if 0 <= q - 1 < PAIRS:
+            if ending:
+                less_bias(2, nc.vector)
+            elif 0 <= q - 1 < PAIRS:
                 weigh(q - 1, 0)
             if live and q > 0:
                 project(q, wv, wvs, "a", a)
@@ -398,85 +401,93 @@ def tile_compressive_memory_update_f1_kernel(
                 x_product(made // C + 1, made % C)
             if q + 1 < PAIRS:
                 logits(q + 1)
-            if made >= last and 0 <= q - 1 < PAIRS:
+            if ending:
+                less_bias(3, nc.vector)
+            elif made >= last and 0 <= q - 1 < PAIRS:
                 weigh(q - 1, 1)
             if live:
                 subtract(q, 0, 2, nc.vector)
                 expo(q, 0)
                 expo(q, 1)
+            if ending:
+                weigh(q - 1, 0)
+                weigh(q - 1, 1)
             if made < last:
                 if q > 0:
                     weigh(q - 1, 1)
             if q % C == 2 and q // C + 1 < NB:
                 x_quant(q // C + 1, 0, C)
-            if 0 <= q - 2 < PAIRS:
+            if q in (12, 13):
+                less_bias(q - 12, nc.vector)
+            if q >= 2 and not ending:
                 sums_out(q - 2)
             if turned < last:
                 x_evac(turned // C + 1, turned % C)
 
-        sums(PAIRS - 1)
-        recip(1)
-        less_bias(0, nc.vector)
-        less_bias(1, nc.vector)
-        less_bias(2, nc.vector)
-        less_bias(3, nc.vector)
+        weigh(PAIRS - 1, 0)
+        sums_out(PAIRS - 3)
+        sums(PAIRS - 2)
+        weigh(PAIRS - 1, 1)
         recip(0)
-        sums_out(PAIRS - 1)
-        pooled(1)
-        recip(3)
+        sums_out(PAIRS - 2)
+        sums(PAIRS - 1)
         pooled(0)
-        pooled(3)
+        recip(1)
+        pooled(1)
         square(0)
-        square(1)
+        sums_out(PAIRS - 1)
         root(0)
         norm(0)
+        recip(3)
+        pooled(3)
+        y_turn(0, "nd")
+        square(1)
+        recip(2)
         square(3)
+        y_evac(0, nc.vector.tensor_copy)
         root(1)
         norm(1)
-        y_turn(0, "nd")
+        y_turn(1, "xt")
+        y_quant(0)
+        second(0, wr, wrs, "z", rr)
+        pooled(2)
         root(3)
         norm(3)
-        recip(2)
-        pooled(2)
-        y_turn(3, "xt")
-        y_evac(0, nc.scalar.copy)
-        y_quant(0)
-        square(2)
-        y_evac(3, nc.vector.tensor_copy)
-        y_turn(1, "nd")
-        y_quant(3)
         y_evac(1, nc.scalar.copy)
-        second(0, wr, wrs, "z", rr)
         gate_in(0)
-        second(0, wu, wus, "a", uu)
-        gate_out(0)
-        y_quant(1)
+        square(2)
         root(2)
+        y_quant(1)
+        second(0, wu, wus, "a", uu)
         norm(2)
-        second(3, wr, wrs, "z", rr)
-        second(1, wu, wus, "a", uu)
-        difference(1)
+        y_turn(3, "nd")
+        gate_out(0)
+        y_evac(3, nc.vector.tensor_copy)
         second(1, wr, wrs, "z", rr)
+        difference(0)
+        gate_in(1)
         y_turn(2, "xt")
         y_evac(2, nc.scalar.copy)
-        gate_in(1)
-        difference(0)
-        gate_out(1)
+        y_quant(3)
         y_quant(2)
+        second(1, wu, wus, "a", uu)
+        difference(1)
         second(3, wu, wus, "a", uu)
-        second(2, wu, wus, "a", uu)
-        mix(0, nc.gpsimd)
-        gate_in(3)
-        second(2, wr, wrs, "z", rr)
         difference(3)
-        store(0, nc.gpsimd)
-        gate_out(3)
-        difference(2)
+        mix(0, nc.gpsimd)
+        second(2, wr, wrs, "z", rr)
+        gate_out(1)
+        mix(1, nc.vector)
         gate_in(2)
+        second(3, wr, wrs, "z", rr)
+        second(2, wu, wus, "a", uu)
+        difference(2)
         gate_out(2)
-        mix(1, nc.gpsimd)
-        mix(3, nc.vector)
-        store(3, nc.vector)
+        gate_in(3)
+        store(0, nc.vector)
         store(1, nc.gpsimd)
+        gate_out(3)
         mix(2, nc.vector)
+        mix(3, nc.vector)
         store(2, nc.vector)
+        store(3, nc.vector)

@@ -128,7 +128,7 @@ def tile_compressive_memory_update_f1_kernel(
         xw, xg, xq, xqs, xt = {}, {}, {}, {}, {}
 
         def x_product(b, i, halves=1):
-            t = cycle([P, D], BF16, "xw", 4)
+            t = cycle([P, D], BF16, "xw", 6)
             n = D // halves
             for h in range(halves):
                 cols = slice(n * h, n * (h + 1))
@@ -241,6 +241,14 @@ def tile_compressive_memory_update_f1_kernel(
                 ee[q] = cycle([P, 2, C, P], F32, "ee", 3)
             nc.scalar.activation(out=ee[q][:, v, :, :], in_=dd[q][:, v, :, :], func=AF.Exp)
 
+        ehalf = {}
+
+        def halve(q):
+            ehalf[q] = cycle([P, 2, 2, P], F32, "ehalf", 2)
+            nc.vector.tensor_tensor(
+                out=ehalf[q][:], in0=ee[q][:, :, 0:2, :], in1=ee[q][:, :, 2:4, :], op=ALU.add
+            )
+
         def weigh(q, v):
             if v == 0:
                 pr[q] = cycle([P, 2, C, P], F32, "pr", 2)
@@ -259,12 +267,13 @@ def tile_compressive_memory_update_f1_kernel(
                 if q % (NCH // 2) == 0:
                     num[b] = keep([P, E], F32, "num%d" % b)
                     den2[b] = keep([P, E], F32, "den%d" % b)
-            src = (pr[q], ee[q])[k]
+            src = (pr[q], ehalf.get(q, ee[q]))[k]
+            terms = 2 if k == 1 and q in ehalf else C
             for v in range(2):
-                for i in range(C):
+                for i in range(terms):
                     nc.tensor.matmul(
                         out=nd[q][:, k, v, :], lhsT=src[:, v, i, :], rhs=ident[:],
-                        start=(i == 0), stop=(i == C - 1), is_transpose=True,
+                        start=(i == 0), stop=(i == terms - 1), is_transpose=True,
                     )
 
         def sums_out(q):
@@ -279,6 +288,9 @@ def tile_compressive_memory_update_f1_kernel(
 
         def less_bias(b, eng):
             eng.tensor_tensor(out=mb[:, b, :], in0=memt[:, b, :], in1=bub[:], op=ALU.subtract)
+
+        def preload():
+            nc.scalar.activation(out=dummy[:], in_=dummy[:], func=AF.Sigmoid)
 
         def recip(b):
             nc.scalar.activation(out=den2[b][:], in_=den2[b][:], func=AF.Abs_reciprocal_sqrt)
@@ -376,118 +388,137 @@ def tile_compressive_memory_update_f1_kernel(
         x_evac(1, 1)
 
         for q in range(PAIRS):
-            live = q < PAIRS
-            made, turned = q + 3, q + 2
+            made, turned = q + 3 + (2 if q > 0 else 0), q + 2
             last = C * (NB - 1)
-
+            if q > 0:
+                project(q, wv, wvs, "a", a)
             if q + 1 < PAIRS:
                 project(q + 1, wz, wzs, "z", z)
-            ending = q == PAIRS - 1
-            if live:
-                max_a(q)
-            if ending:
-                less_bias(2, nc.vector)
-            elif 0 <= q - 1 < PAIRS:
-                weigh(q - 1, 0)
-            if live and q > 0:
-                project(q, wv, wvs, "a", a)
-            if 0 <= q - 2 < PAIRS:
+            if q >= 2:
                 sums(q - 2)
             if turned < last:
                 x_turn(turned // C + 1, turned % C)
-            if live:
-                max_b(q)
-            if made < last:
-                x_product(made // C + 1, made % C)
             if q + 1 < PAIRS:
                 logits(q + 1)
-            if ending:
-                less_bias(3, nc.vector)
-            elif made >= last and 0 <= q - 1 < PAIRS:
-                weigh(q - 1, 1)
-            if live:
+            if q == 0:
+                max_a(q)
+                max_b(q)
+                x_product(made // C + 1, made % C)
                 subtract(q, 0, 2, nc.vector)
                 expo(q, 0)
                 expo(q, 1)
-            if ending:
-                weigh(q - 1, 0)
-                weigh(q - 1, 1)
-            if made < last:
+                for n in range(4, 4 + 2):
+                    x_product(n // C + 1, n % C)
+            elif made < last:
+                max_a(q)
+                if q > 0:
+                    weigh(q - 1, 0)
+                max_b(q)
+                x_product(made // C + 1, made % C)
+                subtract(q, 0, 2, nc.vector)
+                expo(q, 0)
+                expo(q, 1)
                 if q > 0:
                     weigh(q - 1, 1)
-            if q % C == 2 and q // C + 1 < NB:
-                x_quant(q // C + 1, 0, C)
-            if q in (12, 13):
-                less_bias(q - 12, nc.vector)
-            if q >= 2 and not ending:
+                if q % C == 2 and q // C + 1 < NB:
+                    x_quant(q // C + 1, 0, C)
+            elif q < PAIRS - 1:
+                max_a(q)
+                if q > 0:
+                    weigh(q - 1, 0)
+                max_b(q)
+                if q > 0:
+                    weigh(q - 1, 1)
+                subtract(q, 0, 2, nc.vector)
+                expo(q, 0)
+                expo(q, 1)
+                halve(q - 1)
+                if q % C == 2 and q // C + 1 < NB:
+                    x_quant(q // C + 1, 0, C)
+            else:
+                max_a(q)
+                max_b(q)
+                if q > 0:
+                    weigh(q - 1, 0)
+                subtract(q, 0, 2, nc.vector)
+                expo(q, 0)
+                expo(q, 1)
+                if q > 0:
+                    weigh(q - 1, 1)
+            if q >= 2 and q < PAIRS - 1:
                 sums_out(q - 2)
             if turned < last:
                 x_evac(turned // C + 1, turned % C)
 
+        less_bias(0, nc.vector)
         weigh(PAIRS - 1, 0)
-        sums_out(PAIRS - 3)
-        sums(PAIRS - 2)
         weigh(PAIRS - 1, 1)
+        sums_out(PAIRS - 3)
         recip(0)
+        recip(1)
+        sums(PAIRS - 2)
+        less_bias(1, nc.vector)
+        less_bias(3, nc.vector)
         sums_out(PAIRS - 2)
         sums(PAIRS - 1)
         pooled(0)
-        recip(1)
-        pooled(1)
         square(0)
-        sums_out(PAIRS - 1)
+        pooled(1)
+        less_bias(2, nc.vector)
         root(0)
-        norm(0)
-        recip(3)
-        pooled(3)
-        y_turn(0, "nd")
         square(1)
-        recip(2)
-        square(3)
-        y_evac(0, nc.vector.tensor_copy)
+        norm(0)
+        sums_out(PAIRS - 1)
         root(1)
+        recip(3)
         norm(1)
-        y_turn(1, "xt")
+        pooled(3)
+        recip(2)
+        y_turn(0, "nd")
+        y_evac(0, nc.scalar.copy)
         y_quant(0)
-        second(0, wr, wrs, "z", rr)
         pooled(2)
+        y_turn(1, "xt")
+        square(3)
+        second(0, wu, wus, "a", uu)
+        y_evac(1, nc.scalar.copy)
+        square(2)
+        y_quant(1)
+        preload()
+        second(1, wr, wrs, "z", rr)
         root(3)
         norm(3)
-        y_evac(1, nc.scalar.copy)
-        gate_in(0)
-        square(2)
-        root(2)
-        y_quant(1)
-        second(0, wu, wus, "a", uu)
-        norm(2)
         y_turn(3, "nd")
-        gate_out(0)
-        y_evac(3, nc.vector.tensor_copy)
-        second(1, wr, wrs, "z", rr)
         difference(0)
-        gate_in(1)
-        y_turn(2, "xt")
-        y_evac(2, nc.scalar.copy)
-        y_quant(3)
-        y_quant(2)
         second(1, wu, wus, "a", uu)
+        root(2)
+        norm(2)
+        gate_in(1)
+        second(0, wr, wrs, "z", rr)
+        y_evac(3, nc.scalar.copy)
+        y_quant(3)
+        y_turn(2, "xt")
         difference(1)
-        second(3, wu, wus, "a", uu)
-        difference(3)
-        mix(0, nc.gpsimd)
-        second(2, wr, wrs, "z", rr)
-        gate_out(1)
-        mix(1, nc.vector)
-        gate_in(2)
         second(3, wr, wrs, "z", rr)
+        gate_in(0)
+        gate_out(1)
+        y_evac(2, nc.scalar.copy)
+        mix(1, nc.vector)
+        second(3, wu, wus, "a", uu)
+        y_quant(2)
+        second(2, wr, wrs, "z", rr)
+        difference(3)
+        store(1, nc.gpsimd)
+        gate_in(3)
+        gate_in(2)
+        gate_out(0)
         second(2, wu, wus, "a", uu)
         difference(2)
-        gate_out(2)
-        gate_in(3)
-        store(0, nc.vector)
-        store(1, nc.gpsimd)
+        mix(0, nc.gpsimd)
         gate_out(3)
-        mix(2, nc.vector)
         mix(3, nc.vector)
-        store(2, nc.vector)
+        gate_out(2)
+        store(0, nc.vector)
+        mix(2, nc.vector)
         store(3, nc.vector)
+        store(2, nc.vector)

from contextlib import ExitStack

import concourse.mybir as mybir
from concourse.masks import make_identity

F32 = mybir.dt.float32
BF16 = mybir.dt.bfloat16
I32 = mybir.dt.int32
U32 = mybir.dt.uint32
U8 = mybir.dt.uint8
FP8 = mybir.dt.float8_e4m3fn
FP8X4 = mybir.dt.float8_e4m3fn_x4
FP4X4 = mybir.dt.float4_e2m1fn_x4
AF = mybir.ActivationFunctionType
ALU = mybir.AluOpType

T, C, D, E, H = 2048, 4, 1024, 1024, 512
SLOTS = T // C
P = 128
G = D // 512
NB = SLOTS // P
TOK = C * P
NCH = E // P
PAIRS = NB * NCH // 2

BANKS = {"z": 2, "a": 4, "nd": 1, "xt": 1}

FLOPS = 2 * T * D * 2 * E + 2 * SLOTS * E * 2 * H


def tile_compressive_memory_update_f1_kernel(
    tc, x_bytes, x_scale, wv_words, wv_scales, wz_words, wz_scales, pos, gain,
    wu_words, wu_scales, wr_words, wr_scales, bu, br, mem, out,
):
    nc = tc.nc
    with ExitStack() as ctx:
        sb = ctx.enter_context(tc.tile_pool(name="sb", bufs=1))
        ps = ctx.enter_context(tc.psum_pool(name="ps", bufs=2))
        ctx.enter_context(tc.manual_schedule())

        def keep(shape, dtype, name):
            return sb.tile(shape, dtype, name=name, tag=name, bufs=1, align_bytes=64)

        def cycle(shape, dtype, name, bufs):
            return sb.tile(shape, dtype, name=name, tag=name, bufs=bufs, align_bytes=64)

        def bank(shape, dtype, name):
            return ps.tile(shape, dtype, name=name, tag=name, bufs=BANKS[name])

        xv = x_bytes.rearrange("(b j i) k -> b j i k", j=P, i=C)
        xb = []
        for b in range(NB):
            t = keep([P, C, D], U8, "xb%d" % b)
            xb.append(t)
        xs_col = keep([P, G, 8], F32, "xs_col")
        nc.scalar.dma_start(
            out=xs_col[:, :, 0:4], in_=x_scale.rearrange("o (g p t) -> p (o g) t", p=P, t=4)
        )
        for i in range(C):
            nc.sync.dma_start(out=xb[0][:, i, :], in_=xv[0][:, i, :])

        pos_rows = keep([P, P], BF16, "pos_rows")
        nc.vector.memset(pos_rows[:], 0.0)
        nc.scalar.dma_start(out=pos_rows[0 : C * NCH, :], in_=pos.rearrange("i (c p) -> (i c) p", p=P))

        dummy = keep([P, 1], F32, "dummy")
        nc.vector.memset(dummy[:], 0.0)
        nc.scalar.activation(out=dummy[:], in_=dummy[:], func=AF.Exp)

        def load_weight(name, n):
            w = keep([P, G, 2 * n], U8, name)
            plane = keep([P, G, n], U8, name + "_s")
            nc.gpsimd.memset(plane[:].rearrange("p g n -> p (g n)").bitcast(I32), 0)
            return w, plane

        def fetch_scales(plane, scales):
            for q in range(4):
                nc.sync.dma_start(
                    out=plane[32 * q : 32 * q + 4, :, :].bitcast(I32),
                    in_=scales[:, 4 * q : 4 * q + 4, :].rearrange("g q n -> q g n").bitcast(I32),
                )

        def fetch_words(w, words):
            nc.sync.dma_start(out=w[:], in_=words.rearrange("g p n -> p g n"))

        ident = keep([P, P], F32, "ident")
        make_identity(nc, ident[:])
        wz, wzs = load_weight("wz", E)
        wv, wvs = load_weight("wv", E)
        identb = keep([P, P], BF16, "identb")
        make_identity(nc, identb[:])
        wu, wus = load_weight("wu", H)
        wr, wrs = load_weight("wr", H)
        half = keep([P, 1], F32, "half")
        nc.gpsimd.memset(half[:], -0.5)

        fetch_scales(wzs, wz_scales)
        fetch_words(wz, wz_words)
        fetch_scales(wvs, wv_scales)
        fetch_words(wv, wv_words)
        nc.sync.dma_start(out=xb[1][:], in_=xv[1])
        nc.sync.dma_start(out=xb[2][:], in_=xv[2])
        nc.sync.dma_start(out=xb[3][:], in_=xv[3])
        fetch_scales(wus, wu_scales)
        fetch_scales(wrs, wr_scales)
        fetch_words(wu, wu_words)
        fetch_words(wr, wr_words)
        memt = keep([P, NB, H], BF16, "memt")
        nc.sync.dma_start(out=memt[:], in_=mem.rearrange("(b j) h -> j b h", j=P))
        bub = keep([P, H], BF16, "bub")
        nc.sync.dma_start(out=bub[:], in_=bu.partition_broadcast(P))
        brb = keep([P, H], BF16, "brb")
        nc.sync.dma_start(out=brb[:], in_=br.partition_broadcast(P))
        gainb = keep([P, E], BF16, "gainb")
        nc.sync.dma_start(out=gainb[:], in_=gain.partition_broadcast(P))
        mb = keep([P, NB, H], F32, "mb")

        xs = keep([P, D], F32, "xs")
        for g in range(G):
            t = bank([P, 4, P], F32, "z")
            for k in range(4):
                nc.tensor.transpose(t[:, k, :], xs_col[:, g, k : k + 1].to_broadcast([P, P]), ident[:])
            nc.scalar.copy(
                out=xs[:, 512 * g : 512 * (g + 1)].rearrange("p (n t) -> p n t", t=4),
                in_=t[:].rearrange("p t n -> p n t"),
            )

        xw, xg, xq, xqs, xt = {}, {}, {}, {}, {}

        def x_product(b, i, halves=1):
            t = cycle([P, D], BF16, "xw", 6)
            n = D // halves
            for h in range(halves):
                cols = slice(n * h, n * (h + 1))
                nc.vector.tensor_tensor(
                    out=t[:, cols], in0=xb[b][:, i, cols].bitcast(FP8), in1=xs[:, cols], op=ALU.mult
                )
            xw[b, i] = t

        def turn(src, dst):
            words = src[:].bitcast(F32)
            for g in range(G):
                for u in range(2):
                    nc.tensor.transpose(dst[:, g, u, :], words[:, 256 * g + u : 256 * (g + 1) : 2], ident[:])

        def x_turn(b, i, name="xt"):
            if i == 0:
                xg[b] = cycle([P, G, TOK, 2], F32, "xg", 2)
                xq[b] = cycle([P, G, TOK], U32, "xq", 2)
                xqs[b] = cycle([P, G, TOK], U8, "xqs", 2)
            xt[b, i] = bank([P, G, 2, P], F32, name)
            turn(xw[b, i], xt[b, i])

        def x_evac(b, i):
            nc.scalar.copy(
                out=xg[b][:, :, P * i : P * (i + 1), :], in_=xt[b, i][:].rearrange("p g u j -> p g j u")
            )

        def x_quant(b, i0, i1):
            cols = slice(P * i0, P * i1)
            for g in range(G):
                nc.vector.quantize_mx(
                    out=xq[b][:, g, cols].bitcast(FP8X4),
                    scales=xqs[b][:, g, cols],
                    in_=xg[b][:, g, cols, :].rearrange("p n u -> p (n u)").bitcast(BF16),
                )

        z, a, lg, mx1, mx, dd, ee, pr, nd, num, den2 = {}, {}, {}, {}, {}, {}, {}, {}, {}, {}, {}

        def project(q, w, ws, name, dst):
            for v in range(2):
                s = 2 * q + v
                b, c = divmod(s, NCH)
                dst[s] = bank([P, C, P], F32, name)
                for g in range(G):
                    nc.tensor.matmul_mx(
                        out=dst[s][:].rearrange("p i j -> p (i j)"),
                        lhsT=w[:, g, 2 * P * c : 2 * P * (c + 1)].bitcast(FP4X4),
                        lhsT_scale=ws[:, g, P * c : P * (c + 1)],
                        rhs=xq[b][:, g, :].bitcast(FP8X4),
                        rhs_scale=xqs[b][:, g, :],
                        start=(g == 0),
                        stop=(g == G - 1),
                    )

        def project_tile(w, ws, name, dst, i):
            for v in range(2):
                if i == 0:
                    dst[v] = bank([P, C, P], F32, name)
                cols = slice(P * i, P * (i + 1))
                for g in range(G):
                    nc.tensor.matmul_mx(
                        out=dst[v][:, i, :],
                        lhsT=w[:, g, 2 * P * v : 2 * P * (v + 1)].bitcast(FP4X4),
                        lhsT_scale=ws[:, g, P * v : P * (v + 1)],
                        rhs=xq[0][:, g, cols].bitcast(FP8X4),
                        rhs_scale=xqs[0][:, g, cols],
                        start=(g == 0),
                        stop=(g == G - 1),
                    )

        pos_bank = bank([P, P], BF16, "xt")
        nc.tensor.transpose(pos_bank[:], pos_rows[:], identb[:])
        pos_col = keep([P, C * NCH], F32, "pos_col")
        nc.scalar.copy(out=pos_col[:], in_=pos_bank[:, 0 : C * NCH])

        def logits(q, i0=0, i1=C):
            if i0 == 0:
                lg[q] = cycle([P, 2, C, P], F32, "lg", 3)
            for v in range(2):
                s = 2 * q + v
                for i in range(i0, i1):
                    k = i * NCH + s % NCH
                    nc.scalar.activation(
                        out=lg[q][:, v, i, :], in_=z[s][:, i, :], func=AF.Identity,
                        bias=pos_col[:, k : k + 1], scale=1.0,
                    )

        def max_a(q):
            t = cycle([P, 2, 2, P], F32, "mx1", 2)
            nc.vector.tensor_tensor(
                out=t[:], in0=lg[q][:, :, 0:2, :], in1=lg[q][:, :, 2:4, :], op=ALU.max
            )
            mx1[q] = t

        def max_b(q):
            t = cycle([P, 2, P], F32, "mx", 2)
            nc.vector.tensor_tensor(out=t[:], in0=mx1[q][:, :, 0, :], in1=mx1[q][:, :, 1, :], op=ALU.max)
            mx[q] = t

        def subtract(q, v0, v1, eng):
            if q not in dd:
                dd[q] = cycle([P, 2, C, P], F32, "dd", 2)
            eng.tensor_tensor(
                out=dd[q][:, v0:v1, :, :], in0=lg[q][:, v0:v1, :, :],
                in1=mx[q][:, v0:v1, :].unsqueeze(2).to_broadcast([P, v1 - v0, C, P]), op=ALU.subtract,
            )

        def expo(q, v):
            if q not in ee:
                ee[q] = cycle([P, 2, C, P], F32, "ee", 3)
            nc.scalar.activation(out=ee[q][:, v, :, :], in_=dd[q][:, v, :, :], func=AF.Exp)

        ehalf = {}

        def halve(q):
            ehalf[q] = cycle([P, 2, 2, P], F32, "ehalf", 2)
            nc.vector.tensor_tensor(
                out=ehalf[q][:], in0=ee[q][:, :, 0:2, :], in1=ee[q][:, :, 2:4, :], op=ALU.add
            )

        def weigh(q, v):
            if v == 0:
                pr[q] = cycle([P, 2, C, P], F32, "pr", 2)
            nc.vector.tensor_tensor(
                out=pr[q][:, v, :, :], in0=ee[q][:, v, :, :], in1=a[2 * q + v][:], op=ALU.mult
            )

        def sums(q, k=None):
            if k is None:
                sums(q, 0)
                sums(q, 1)
                return
            b = q // (NCH // 2)
            if k == 0:
                nd[q] = bank([P, 2, 2, P], F32, "nd")
                if q % (NCH // 2) == 0:
                    num[b] = keep([P, E], F32, "num%d" % b)
                    den2[b] = keep([P, E], F32, "den%d" % b)
            src = (pr[q], ehalf.get(q, ee[q]))[k]
            terms = 2 if k == 1 and q in ehalf else C
            for v in range(2):
                for i in range(terms):
                    nc.tensor.matmul(
                        out=nd[q][:, k, v, :], lhsT=src[:, v, i, :], rhs=ident[:],
                        start=(i == 0), stop=(i == terms - 1), is_transpose=True,
                    )

        def sums_out(q):
            b, c = divmod(q, NCH // 2)
            cols = slice(2 * P * c, 2 * P * (c + 1))
            nc.scalar.copy(out=num[b][:, cols], in_=nd[q][:, 0, :, :].rearrange("p v n -> p (v n)"))
            nc.scalar.activation(
                out=den2[b][:, cols], in_=nd[q][:, 1, :, :].rearrange("p v n -> p (v n)"), func=AF.Square
            )

        yy, yt, yg, yq, yqs, uu, rr, ssq, rsd, gate, diff, frac = {}, {}, {}, {}, {}, {}, {}, {}, {}, {}, {}, {}

        def less_bias(b, eng):
            eng.tensor_tensor(out=mb[:, b, :], in0=memt[:, b, :], in1=bub[:], op=ALU.subtract)

        def preload():
            nc.scalar.activation(out=dummy[:], in_=dummy[:], func=AF.Sigmoid)

        def recip(b):
            nc.scalar.activation(out=den2[b][:], in_=den2[b][:], func=AF.Abs_reciprocal_sqrt)

        def pooled(b):
            nc.vector.tensor_tensor(out=num[b][:], in0=num[b][:], in1=den2[b][:], op=ALU.mult)

        def square(b):
            junk = cycle([P, E], BF16, "junk", 1)
            ssq[b] = keep([P, 1], F32, "ssq%d" % b)
            nc.scalar.activation(
                out=junk[:], in_=num[b][:], func=AF.Square, scale=1.0 / 32.0, accum_out=ssq[b][:]
            )

        def root(b):
            rsd[b] = keep([P, 1], F32, "rsd%d" % b)
            nc.gpsimd.tensor_tensor(out=rsd[b][:], in0=ssq[b][:], in1=half[:], op=ALU.pow)

        def norm(b):
            yy[b] = cycle([P, E], BF16, "yy", 2)
            nc.vector.scalar_tensor_tensor(
                out=yy[b][:], in0=num[b][:], scalar=rsd[b][:], in1=gainb[:], op0=ALU.mult, op1=ALU.mult
            )

        def y_turn(b, name):
            yt[b] = bank([P, G, 2, P], F32, name)
            turn(yy[b], yt[b])

        def y_evac(b, copy):
            yg[b] = cycle([P, G, P, 2], F32, "yg", 2)
            copy(out=yg[b][:], in_=yt[b][:].rearrange("p g u j -> p g j u"))

        def y_quant(b):
            yq[b] = cycle([P, G * P], U32, "yq", 3)
            yqs[b] = cycle([P, G * P], U8, "yqs", 3)
            nc.vector.quantize_mx(
                out=yq[b][:].bitcast(FP8X4), scales=yqs[b][:],
                in_=yg[b][:].rearrange("p g n u -> p (g n u)").bitcast(BF16),
            )

        def second(b, w, ws, name, dst):
            dst[b] = bank([P, H], F32, name)
            for g in range(G):
                cols = slice(P * g, P * (g + 1))
                nc.tensor.matmul_mx(
                    out=dst[b][:], lhsT=yq[b][:, cols].bitcast(FP8X4), lhsT_scale=yqs[b][:, cols],
                    rhs=w[:, g, :].bitcast(FP4X4), rhs_scale=ws[:, g, :],
                    start=(g == 0), stop=(g == G - 1),
                )

        def gate_in(b):
            gate[b] = cycle([P, H], F32, "gate", 4)
            nc.vector.tensor_tensor(out=gate[b][:], in0=rr[b][:], in1=brb[:], op=ALU.add)

        def gate_out(b):
            nc.scalar.activation(out=gate[b][:], in_=gate[b][:], func=AF.Sigmoid, scale=-1.0)

        def difference(b):
            diff[b] = cycle([P, H], F32, "diff", 4)
            nc.vector.tensor_tensor(out=diff[b][:], in0=uu[b][:], in1=mb[:, b, :], op=ALU.subtract)

        def mix(b, eng):
            eng.tensor_tensor(out=diff[b][:], in0=gate[b][:], in1=diff[b][:], op=ALU.mult)

        def store(b, eng):
            o = cycle([P, H], F32, "o", 4)
            eng.tensor_tensor(out=o[:], in0=diff[b][:], in1=memt[:, b, :], op=ALU.add)
            nc.sync.dma_start(out=out[P * b : P * (b + 1), :], in_=o[:])

        names = ("a", "a", "nd", "xt")

        def begin(i, w, ws, name, dst):
            project_tile(w, ws, name, dst, i)

        for i in range(C):
            x_product(0, i, 2)
            if i > 0:
                x_quant(0, i - 1, i)
            x_turn(0, i, names[i])
            x_evac(0, i)
            if i > 1:
                begin(i - 2, wz, wzs, "z", z)
                logits(0, i - 2, i - 1)
        x_product(1, 0)
        x_quant(0, 3, 4)
        for i in (2, 3):
            begin(i, wz, wzs, "z", z)
            logits(0, i, i + 1)
        project(0, wv, wvs, "a", a)
        x_product(1, 1)
        x_turn(1, 0)
        x_evac(1, 0)
        x_product(1, 2)
        x_turn(1, 1)
        x_evac(1, 1)

        for q in range(PAIRS):
            made, turned = q + 3 + (2 if q > 0 else 0), q + 2
            last = C * (NB - 1)
            if q > 0:
                project(q, wv, wvs, "a", a)
            if q + 1 < PAIRS:
                project(q + 1, wz, wzs, "z", z)
            if q >= 2:
                sums(q - 2)
            if turned < last:
                x_turn(turned // C + 1, turned % C)
            if q + 1 < PAIRS:
                logits(q + 1)
            if q == 0:
                max_a(q)
                max_b(q)
                x_product(made // C + 1, made % C)
                subtract(q, 0, 2, nc.vector)
                expo(q, 0)
                expo(q, 1)
                for n in range(4, 4 + 2):
                    x_product(n // C + 1, n % C)
            elif made < last:
                max_a(q)
                if q > 0:
                    weigh(q - 1, 0)
                max_b(q)
                x_product(made // C + 1, made % C)
                subtract(q, 0, 2, nc.vector)
                expo(q, 0)
                expo(q, 1)
                if q > 0:
                    weigh(q - 1, 1)
                if q % C == 2 and q // C + 1 < NB:
                    x_quant(q // C + 1, 0, C)
            elif q < PAIRS - 1:
                max_a(q)
                if q > 0:
                    weigh(q - 1, 0)
                max_b(q)
                if q > 0:
                    weigh(q - 1, 1)
                subtract(q, 0, 2, nc.vector)
                expo(q, 0)
                expo(q, 1)
                halve(q - 1)
                if q % C == 2 and q // C + 1 < NB:
                    x_quant(q // C + 1, 0, C)
            else:
                max_a(q)
                max_b(q)
                if q > 0:
                    weigh(q - 1, 0)
                subtract(q, 0, 2, nc.vector)
                expo(q, 0)
                expo(q, 1)
                if q > 0:
                    weigh(q - 1, 1)
            if q >= 2 and q < PAIRS - 1:
                sums_out(q - 2)
            if turned < last:
                x_evac(turned // C + 1, turned % C)

        less_bias(0, nc.vector)
        weigh(PAIRS - 1, 0)
        weigh(PAIRS - 1, 1)
        sums_out(PAIRS - 3)
        recip(0)
        recip(1)
        sums(PAIRS - 2)
        less_bias(1, nc.vector)
        less_bias(3, nc.vector)
        sums_out(PAIRS - 2)
        sums(PAIRS - 1)
        pooled(0)
        square(0)
        pooled(1)
        less_bias(2, nc.vector)
        root(0)
        square(1)
        norm(0)
        sums_out(PAIRS - 1)
        root(1)
        recip(3)
        norm(1)
        pooled(3)
        recip(2)
        y_turn(0, "nd")
        y_evac(0, nc.scalar.copy)
        y_quant(0)
        pooled(2)
        y_turn(1, "xt")
        square(3)
        second(0, wu, wus, "a", uu)
        y_evac(1, nc.scalar.copy)
        square(2)
        y_quant(1)
        preload()
        second(1, wr, wrs, "z", rr)
        root(3)
        norm(3)
        y_turn(3, "nd")
        difference(0)
        second(1, wu, wus, "a", uu)
        root(2)
        norm(2)
        gate_in(1)
        second(0, wr, wrs, "z", rr)
        y_evac(3, nc.scalar.copy)
        y_quant(3)
        y_turn(2, "xt")
        difference(1)
        second(3, wr, wrs, "z", rr)
        gate_in(0)
        gate_out(1)
        y_evac(2, nc.scalar.copy)
        mix(1, nc.vector)
        second(3, wu, wus, "a", uu)
        y_quant(2)
        second(2, wr, wrs, "z", rr)
        difference(3)
        store(1, nc.gpsimd)
        gate_in(3)
        gate_in(2)
        gate_out(0)
        second(2, wu, wus, "a", uu)
        difference(2)
        mix(0, nc.gpsimd)
        gate_out(3)
        mix(3, nc.vector)
        gate_out(2)
        store(0, nc.vector)
        mix(2, nc.vector)
        store(3, nc.vector)
        store(2, nc.vector)
